import numpy as np
import ml_dtypes


def mxq(x, axis, fmt="e4m3"):
    dtype, down = {"e4m3": (ml_dtypes.float8_e4m3fn, 7), "e5m2": (ml_dtypes.float8_e5m2, 14)}[fmt]
    v = np.moveaxis(np.asarray(x, np.float32).astype(ml_dtypes.bfloat16).astype(np.float64), axis, -1)
    blocks = v.reshape(v.shape[:-1] + (-1, 32))
    amax = np.abs(blocks).max(-1, keepdims=True)
    byte = np.maximum(np.where(amax > 0, np.frexp(amax)[1] - 1 + 127, 0) - down, 1)
    scale = np.exp2(byte - 127.0)
    codes = (blocks / scale).astype(np.float32).astype(dtype).astype(np.float64)
    return np.moveaxis((codes * scale).reshape(v.shape), -1, axis)


WIDE = False


def mx_kscale(k):
    if not WIDE:
        return np.ones(k)
    levels = np.array([10, -10, 5, -5, 0])
    if k % 512:
        return np.exp2(np.random.permutation(np.resize(levels, k // 32))).repeat(32)
    a = np.empty((k // 512, 16))
    for p in range(k // 512):
        a[p, :8] = np.random.permutation(np.resize(levels, 8))
        for g in range(8):
            far = levels[np.abs(levels - a[p, g]) >= 10]
            a[p, g + 8] = far[np.random.randint(len(far))]
    return np.exp2(a.ravel()).repeat(32)


def f64(x):
    return np.asarray(x).astype(np.float64)


def striped(idx):
    return np.tile(np.asarray(idx).reshape(-1, 16).T, (8, 1)).astype(np.uint16)


def unstriped(offs):
    return offs[:16].T.reshape(-1).astype(np.int64)


E2M1 = np.array([0.0, 0.5, 1.0, 1.5, 2.0, 3.0, 4.0, 6.0, -0.0, -0.5, -1.0, -1.5, -2.0, -3.0, -4.0, -6.0])


def pack_weight(w, fmt):
    k, n = w.shape
    w = f64(np.asarray(w, np.float32).astype(ml_dtypes.bfloat16)).reshape(k // 32, 32, n)
    amax = np.abs(w).max(1)
    if fmt == "e4m3":
        byte = np.frexp(amax)[1] - 1 + 127 - 7
    else:
        mant, ex = np.frexp(amax / 6.0)
        byte = np.where(mant > 0.5, ex, ex - 1) + 127
    byte = np.clip(np.where(amax > 0, byte, 1), 1, 254)
    scaled = (w * np.exp2(127.0 - byte)[:, None, :]).reshape(k, n).astype(np.float32)
    by_word = np.ascontiguousarray(scaled.reshape(k // 512, 128, 4, n).transpose(0, 1, 3, 2))
    if fmt == "e4m3":
        words = by_word.astype(ml_dtypes.float8_e4m3fn).view(np.uint8)
    else:
        c = by_word.astype(ml_dtypes.float4_e2m1fn).view(np.uint8) & 0xF
        words = (c[..., 0::2] | (c[..., 1::2] << 4)).reshape(k // 512, 128, 2 * n)
    return np.ascontiguousarray(words), np.ascontiguousarray(byte.astype(np.uint8).reshape(k // 512, 16, n))


def unpack_weight(words, scales, fmt):
    g, _, n = scales.shape
    words = np.ascontiguousarray(words).reshape(g, 128, n, -1)
    if fmt == "e4m3":
        vals = words.view(ml_dtypes.float8_e4m3fn).astype(np.float64)
    else:
        nib = np.empty((g, 128, n, 4), np.uint8)
        nib[..., 0::2] = words & 0xF
        nib[..., 1::2] = words >> 4
        vals = E2M1[nib]
    vals = vals * np.repeat(np.exp2(scales.astype(np.float64) - 127.0), 8, axis=1)[..., None]
    return vals.transpose(0, 1, 3, 2).reshape(g * 512, n)


D, T, I, Q, E = 512, 2048, 512, 128, 512


def setup_inputs():
    n = np.random.standard_normal
    idx = np.random.permutation(T)[:I]
    fd = mx_kscale(D)
    fi = mx_kscale(I)
    ti = np.ones(T)
    ti[idx] = fi
    keysp = pack_weight(n((D, T)) / fd[:, None], "e4m3")
    return {
        "query": (n((D, Q)) * 0.25 / np.sqrt(D) * fd[:, None]).astype(np.float32),
        "keys_words": keysp[0],
        "keys_scales": keysp[1],
        "m0": (np.random.uniform(0.3, 1.2, (Q, 1))).astype(np.float32),
        "z0": (np.random.uniform(100.0, 500.0, (Q, 1))).astype(np.float32),
        "o0": (n((Q, E)) * 0.06).astype(np.float32),
        "size": (np.random.uniform(0.5, 2.0, (1, I)) * fi).astype(np.float32),
        "vals": (n((E, T)) / ti).astype(np.float32),
        "offs": striped(idx),
    }


def reference(query, keys_words, keys_scales, m0, z0, o0, size, vals, offs):
    idx = unstriped(offs)
    keysu = unpack_weight(keys_words, keys_scales, "e4m3")
    queryq = mxq(f64(query), 0, "e4m3")
    keysidxg = keysu[:, idx]
    a = queryq.T @ keysidxg
    m1 = np.maximum(np.max(a, axis=1, keepdims=True), f64(m0))
    p = np.exp(a - m1)
    r0 = f64(z0) * np.exp(f64(m0) - m1)
    z = np.sum(p, axis=1, keepdims=True) + r0
    w = p * f64(size)
    wt = w.T
    vt = f64(vals)[:, idx].T
    wtq = mxq(wt, 0, "e4m3")
    vtq = mxq(vt, 0, "e4m3")
    o = wtq.T @ vtq
    y = (o + f64(o0) * r0) / z
    return y

@@ -1,0 +1,154 @@
+from contextlib import ExitStack
+
+import concourse.mybir as mybir
+from concourse.masks import make_identity
+
+D, T, I, Q, E = 512, 2048, 512, 128, 512
+FLOPS = 2 * D * Q * I + 2 * I * Q * E
+
+F32 = mybir.dt.float32
+BF16 = mybir.dt.bfloat16
+I32 = mybir.dt.int32
+U32 = mybir.dt.uint32
+U16 = mybir.dt.uint16
+U8 = mybir.dt.uint8
+FP8X4 = mybir.dt.float8_e4m3fn_x4
+ALU = mybir.AluOpType
+ACT = mybir.ActivationFunctionType
+
+P = 128
+PACK = 4
+BLOCKS = E // P
+
+
+def tile_attend_resumedread_kernel(tc, query, keys_words, keys_scales, m0, z0, o0, size, vals, offs, out):
+    nc = tc.nc
+    with ExitStack() as ctx:
+        keep = ctx.enter_context(tc.tile_pool(name="keep", bufs=1))
+        psum = ctx.enter_context(tc.psum_pool(name="psum", bufs=1))
+
+        key_words = keep.tile([P, T], U32, name="key_words", align_bytes=64)
+        key_scales = keep.tile([P, T], U8, name="key_scales", align_bytes=64)
+        offsets = keep.tile([P, I // 16], U16, name="offsets")
+        q_raw = keep.tile([P, PACK, Q], F32, name="q_raw")
+        v_raw = [keep.tile([P, T], F32, name="v_raw%d" % b, align_bytes=64) for b in range(BLOCKS)]
+        o_old = keep.tile([P, E], F32, name="o_old")
+        m_old = keep.tile([P, 1], F32, name="m_old")
+        z_old = keep.tile([P, 1], F32, name="z_old")
+        size_col = keep.tile([P, PACK], F32, name="size_col")
+        ident = keep.tile([P, P], F32, name="ident")
+        warm = keep.tile([P, 1], F32, name="warm")
+        warm_out = keep.tile([P, 1], F32, name="warm_out")
+
+        nc.vector.memset(key_scales[:].bitcast(I32), 0)
+        nc.vector.memset(warm[:], 0.0)
+        nc.scalar.activation(warm_out[:], warm[:], ACT.Exp)
+
+        nc.sync.dma_start(out=key_words[:].bitcast(I32),
+                          in_=keys_words[0].rearrange("p n t -> p (n t)").bitcast(I32))
+        for quad in range(4):
+            nc.sync.dma_start(out=key_scales[32 * quad : 32 * quad + 4, :].bitcast(I32),
+                              in_=keys_scales[0, 4 * quad : 4 * quad + 4, :].bitcast(I32))
+        nc.sync.dma_start(offsets[:], offs)
+        nc.sync.dma_start(out=q_raw[:], in_=query.rearrange("(p j) q -> p j q", j=PACK))
+        nc.sync.dma_start(out=v_raw[0][:], in_=vals[0:P, :])
+        nc.sync.dma_start(out=m_old[:], in_=m0)
+        nc.sync.dma_start(out=size_col[:], in_=size[0].rearrange("(p j) -> p j", j=PACK))
+        nc.sync.dma_start(out=z_old[:], in_=z0)
+        for b in range(1, BLOCKS):
+            nc.sync.dma_start(out=v_raw[b][:], in_=vals[b * P : (b + 1) * P, :])
+        nc.sync.dma_start(out=o_old[:], in_=o0)
+        make_identity(nc, ident[:])
+
+        q_bf = keep.tile([P, Q, PACK], BF16, name="q_bf", align_bytes=64)
+        q_codes = keep.tile([P, Q], U32, name="q_codes", align_bytes=64)
+        q_scales = keep.tile([P, Q], U8, name="q_scales", align_bytes=64)
+        k_codes = keep.tile([P, I], U32, name="k_codes", align_bytes=64)
+        k_scales = keep.tile([P, I], U8, name="k_scales", align_bytes=64)
+        nc.scalar.copy(out=q_bf[:], in_=q_raw[:].rearrange("p j q -> p q j"))
+        nc.vector.tensor_copy(k_codes[:], key_words[:].indirect(offsets[:]))
+        nc.vector.quantize_mx(out=q_codes[:].bitcast(FP8X4), scales=q_scales[:],
+                              in_=q_bf[:].rearrange("p q j -> p (q j)"))
+        nc.vector.tensor_copy(k_scales[:], key_scales[:].indirect(offsets[:]))
+
+        scores = psum.tile([P, I], F32, name="scores")
+        nc.tensor.matmul_mx(out=scores[:], lhsT=q_codes[:].bitcast(FP8X4), lhsT_scale=q_scales[:],
+                            rhs=k_codes[:].bitcast(FP8X4), rhs_scale=k_scales[:], start=True, stop=True)
+
+        neg_m_old = keep.tile([P, 1], F32, name="neg_m_old")
+        neg_m = keep.tile([P, 1], F32, name="neg_m")
+        neg_scores = keep.tile([P, PACK, P], F32, name="neg_scores")
+        p_dealt = keep.tile([P, PACK, P], F32, name="p_dealt")
+        p_sum = keep.tile([P, 1], F32, name="p_sum")
+        decay = keep.tile([P, 1], F32, name="decay")
+        r_old = keep.tile([P, 1], F32, name="r_old")
+        z_new = keep.tile([P, 1], F32, name="z_new")
+        inv_z = keep.tile([P, 1], F32, name="inv_z")
+        old_share = keep.tile([P, 1], F32, name="old_share")
+        o_carried = keep.tile([P, E], F32, name="o_carried")
+        nc.scalar.activation(neg_m_old[:], m_old[:], ACT.Copy, scale=-1.0)
+
+        v_codes = []
+        v_scales = []
+
+        def value_block(b):
+            v_picked = keep.tile([P, I], BF16, name="v_picked%d" % b, align_bytes=64)
+            nc.vector.tensor_copy(v_picked[:], v_raw[b][:].indirect(offsets[:]))
+            pairs = v_picked[:].bitcast(F32)
+            turned = psum.tile([P, 2, P], F32, name="turned%d" % b)
+            for u in range(2):
+                nc.tensor.transpose(turned[:, u, :], pairs[:, u : I // 2 : 2], ident[:])
+            v_bf = keep.tile([P, P * PACK], BF16, name="v_bf%d" % b, align_bytes=64)
+            nc.scalar.copy(out=v_bf[:].bitcast(F32).rearrange("p (e u) -> p e u", u=2),
+                           in_=turned[:].rearrange("p u e -> p e u"))
+            codes = keep.tile([P, P], U32, name="v_codes%d" % b, align_bytes=64)
+            scales = keep.tile([P, P], U8, name="v_scales%d" % b, align_bytes=64)
+            nc.vector.quantize_mx(out=codes[:].bitcast(FP8X4), scales=scales[:], in_=v_bf[:])
+            v_codes.append(codes)
+            v_scales.append(scales)
+
+        nc.vector.tensor_scalar(out=neg_scores[:], in0=scores[:].rearrange("q (s t) -> q t s", t=PACK),
+                                scalar1=-1.0, scalar2=neg_m_old[:], op0=ALU.mult, op1=ALU.min,
+                                accum_out=neg_m[:])
+        value_block(0)
+        nc.scalar.activation(p_dealt[:], neg_scores[:], ACT.Exp, bias=neg_m[:], scale=-1.0, accum_out=p_sum[:])
+        nc.scalar.activation(decay[:], m_old[:], ACT.Exp, bias=neg_m[:])
+        nc.scalar.activation(r_old[:], decay[:], ACT.Copy, scale=z_old[:])
+        nc.scalar.activation(z_new[:], decay[:], ACT.Identity, bias=p_sum[:], scale=z_old[:])
+
+        p_turned = psum.tile([P, PACK, Q], F32, name="p_turned")
+        for t in range(PACK):
+            nc.tensor.transpose(p_turned[:, t, :], p_dealt[:, t, :], ident[:])
+        w_bf = keep.tile([P, Q, PACK], BF16, name="w_bf", align_bytes=64)
+        w_codes = keep.tile([P, Q], U32, name="w_codes", align_bytes=64)
+        w_scales = keep.tile([P, Q], U8, name="w_scales", align_bytes=64)
+        nc.vector.tensor_tensor(out=w_bf[:], in0=p_turned[:].rearrange("s t q -> s q t"),
+                                in1=size_col[:].unsqueeze(1).to_broadcast([P, Q, PACK]), op=ALU.mult)
+        nc.vector.reciprocal(inv_z[:], z_new[:])
+        nc.vector.quantize_mx(out=w_codes[:].bitcast(FP8X4), scales=w_scales[:],
+                              in_=w_bf[:].rearrange("p q j -> p (q j)"))
+        nc.scalar.activation(old_share[:], r_old[:], ACT.Copy, scale=inv_z[:])
+        value_block(1)
+        value_block(2)
+
+        early = (BLOCKS - 1) * P
+        o_early = psum.tile([P, early], F32, name="o_early")
+        o_last = psum.tile([P, P], F32, name="o_last")
+        y_early = keep.tile([P, early], F32, name="y_early")
+        y_last = keep.tile([P, P], F32, name="y_last")
+
+        def product(dst, b):
+            nc.tensor.matmul_mx(out=dst, lhsT=w_codes[:].bitcast(FP8X4), lhsT_scale=w_scales[:],
+                                rhs=v_codes[b][:].bitcast(FP8X4), rhs_scale=v_scales[b][:], start=True, stop=True)
+
+        for b in range(BLOCKS - 1):
+            product(o_early[:, b * P : (b + 1) * P], b)
+        value_block(BLOCKS - 1)
+        nc.scalar.activation(o_carried[:], o_old[:], ACT.Copy, scale=old_share[:])
+        nc.vector.scalar_tensor_tensor(out=y_early[:], in0=o_early[:], scalar=inv_z[:], in1=o_carried[:, :early],
+                                       op0=ALU.mult, op1=ALU.add)
+        nc.sync.dma_start(out=out[:, :early], in_=y_early[:])
+        product(o_last[:], BLOCKS - 1)
+        nc.vector.scalar_tensor_tensor(out=y_last[:], in0=o_last[:], scalar=inv_z[:], in1=o_carried[:, early:],
+                                       op0=ALU.mult, op1=ALU.add)
+        nc.sync.dma_start(out=out[:, early:], in_=y_last[:])

@@ -28,10 +28,10 @@ def tile_attend_resumedread_kernel(tc, query, keys_words, keys_scales, m0, z0, o
         psum = ctx.enter_context(tc.psum_pool(name="psum", bufs=1))
 
         key_words = keep.tile([P, T], U32, name="key_words", align_bytes=64)
-        key_scales = keep.tile([P, T], U8, name="key_scales", align_bytes=64)
+        key_scales = keep.tile([P, T], U8, name="key_scales", tag="key_scales", align_bytes=64)
         offsets = keep.tile([P, I // 16], U16, name="offsets")
         q_raw = keep.tile([P, PACK, Q], F32, name="q_raw")
-        v_raw = [keep.tile([P, T], F32, name="v_raw%d" % b, align_bytes=64) for b in range(BLOCKS)]
+        v_raw = [keep.tile([P, T], F32, name="v_raw%d" % b, tag="v_raw%d" % b, align_bytes=64) for b in range(BLOCKS)]
         o_old = keep.tile([P, E], F32, name="o_old")
         m_old = keep.tile([P, 1], F32, name="m_old")
         z_old = keep.tile([P, 1], F32, name="z_old")
@@ -61,23 +61,23 @@ def tile_attend_resumedread_kernel(tc, query, keys_words, keys_scales, m0, z0, o
         make_identity(nc, ident[:])
 
         q_bf = keep.tile([P, Q, PACK], BF16, name="q_bf", align_bytes=64)
-        q_codes = keep.tile([P, Q], U32, name="q_codes", align_bytes=64)
         q_scales = keep.tile([P, Q], U8, name="q_scales", align_bytes=64)
         k_codes = keep.tile([P, I], U32, name="k_codes", align_bytes=64)
         k_scales = keep.tile([P, I], U8, name="k_scales", align_bytes=64)
         nc.scalar.copy(out=q_bf[:], in_=q_raw[:].rearrange("p j q -> p q j"))
         nc.vector.tensor_copy(k_codes[:], key_words[:].indirect(offsets[:]))
+        nc.vector.tensor_copy(k_scales[:], key_scales[:].indirect(offsets[:]))
+        q_codes = keep.tile([P, Q], U32, name="q_codes", align_bytes=64)
         nc.vector.quantize_mx(out=q_codes[:].bitcast(FP8X4), scales=q_scales[:],
                               in_=q_bf[:].rearrange("p q j -> p (q j)"))
-        nc.vector.tensor_copy(k_scales[:], key_scales[:].indirect(offsets[:]))
 
-        scores = psum.tile([P, I], F32, name="scores")
+        scores = psum.tile([P, I], F32, name="scores", tag="turned0")
         nc.tensor.matmul_mx(out=scores[:], lhsT=q_codes[:].bitcast(FP8X4), lhsT_scale=q_scales[:],
                             rhs=k_codes[:].bitcast(FP8X4), rhs_scale=k_scales[:], start=True, stop=True)
 
-        neg_m_old = keep.tile([P, 1], F32, name="neg_m_old")
+        neg_m_old = keep.tile([P, 1], F32, name="neg_m_old", tag="after_max2", align_bytes=64)
         neg_m = keep.tile([P, 1], F32, name="neg_m")
-        neg_scores = keep.tile([P, PACK, P], F32, name="neg_scores")
+        neg_scores = keep.tile([P, I], BF16, name="neg_scores", tag="after_max", align_bytes=64)
         p_dealt = keep.tile([P, PACK, P], F32, name="p_dealt")
         p_sum = keep.tile([P, 1], F32, name="p_sum")
         decay = keep.tile([P, 1], F32, name="decay")
@@ -85,70 +85,77 @@ def tile_attend_resumedread_kernel(tc, query, keys_words, keys_scales, m0, z0, o
         z_new = keep.tile([P, 1], F32, name="z_new")
         inv_z = keep.tile([P, 1], F32, name="inv_z")
         old_share = keep.tile([P, 1], F32, name="old_share")
-        o_carried = keep.tile([P, E], F32, name="o_carried")
-        nc.scalar.activation(neg_m_old[:], m_old[:], ACT.Copy, scale=-1.0)
+        nc.gpsimd.tensor_scalar(out=neg_m_old[:], in0=m_old[:], scalar1=-1.0, scalar2=0.0, op0=ALU.mult, op1=ALU.add)
 
-        v_codes = []
-        v_scales = []
-
-        def value_block(b):
-            v_picked = keep.tile([P, I], BF16, name="v_picked%d" % b, align_bytes=64)
+        def pick(b, picked_tag):
+            v_picked = keep.tile([P, I], BF16, name="v_picked%d" % b, tag=picked_tag, align_bytes=64)
             nc.vector.tensor_copy(v_picked[:], v_raw[b][:].indirect(offsets[:]))
-            pairs = v_picked[:].bitcast(F32)
-            turned = psum.tile([P, 2, P], F32, name="turned%d" % b)
-            for u in range(2):
-                nc.tensor.transpose(turned[:, u, :], pairs[:, u : I // 2 : 2], ident[:])
-            v_bf = keep.tile([P, P * PACK], BF16, name="v_bf%d" % b, align_bytes=64)
-            nc.scalar.copy(out=v_bf[:].bitcast(F32).rearrange("p (e u) -> p e u", u=2),
-                           in_=turned[:].rearrange("p u e -> p e u"))
-            codes = keep.tile([P, P], U32, name="v_codes%d" % b, align_bytes=64)
-            scales = keep.tile([P, P], U8, name="v_scales%d" % b, align_bytes=64)
-            nc.vector.quantize_mx(out=codes[:].bitcast(FP8X4), scales=scales[:], in_=v_bf[:])
-            v_codes.append(codes)
-            v_scales.append(scales)
+            return v_picked
 
-        nc.vector.tensor_scalar(out=neg_scores[:], in0=scores[:].rearrange("q (s t) -> q t s", t=PACK),
-                                scalar1=-1.0, scalar2=neg_m_old[:], op0=ALU.mult, op1=ALU.min,
-                                accum_out=neg_m[:])
-        value_block(0)
-        nc.scalar.activation(p_dealt[:], neg_scores[:], ACT.Exp, bias=neg_m[:], scale=-1.0, accum_out=p_sum[:])
+        def turn(name, picked, bank_tag):
+            n = len(picked)
+            turned = psum.tile([P, n, 2, P], F32, name="turned" + name, tag=bank_tag)
+            for j, v_picked in enumerate(picked):
+                pairs = v_picked[:].bitcast(F32)
+                for u in range(2):
+                    nc.tensor.transpose(turned[:, j, u, :], pairs[:, u : I // 2 : 2], ident[:])
+            v_bf = keep.tile([P, n * P * PACK], BF16, name="v_bf" + name, tag="v_bf" + name, align_bytes=64)
+            nc.scalar.copy(out=v_bf[:].bitcast(F32).rearrange("p (j e u) -> p j e u", j=n, u=2),
+                           in_=turned[:].rearrange("p j u e -> p j e u"))
+            return v_bf
+
+        def quantise(name, src, codes_tag):
+            width = src.shape[1] // PACK
+            codes = keep.tile([P, width], U32, name=name + "_codes", tag=codes_tag, align_bytes=64)
+            scales = keep.tile([P, width], U8, name=name + "_scales", align_bytes=64)
+            nc.vector.quantize_mx(out=codes[:].bitcast(FP8X4), scales=scales[:], in_=src)
+            return codes[:], scales[:]
+
+        nc.vector.tensor_scalar(out=neg_scores[:], in0=scores[:], scalar1=-1.0, scalar2=neg_m_old[:],
+                                op0=ALU.mult, op1=ALU.min, accum_out=neg_m[:])
+        nc.scalar.activation(p_dealt[:], scores[:].rearrange("q (s t) -> q t s", t=PACK), ACT.Exp,
+                             bias=neg_m[:], accum_out=p_sum[:])
         nc.scalar.activation(decay[:], m_old[:], ACT.Exp, bias=neg_m[:])
         nc.scalar.activation(r_old[:], decay[:], ACT.Copy, scale=z_old[:])
         nc.scalar.activation(z_new[:], decay[:], ACT.Identity, bias=p_sum[:], scale=z_old[:])
-
         p_turned = psum.tile([P, PACK, Q], F32, name="p_turned")
         for t in range(PACK):
             nc.tensor.transpose(p_turned[:, t, :], p_dealt[:, t, :], ident[:])
+
+        v_picked0 = pick(0, "after_max")
+        v_picked1 = pick(1, "after_max2")
+        v_bf01 = turn("01", [v_picked0, v_picked1], "turned0")
+
         w_bf = keep.tile([P, Q, PACK], BF16, name="w_bf", align_bytes=64)
-        w_codes = keep.tile([P, Q], U32, name="w_codes", align_bytes=64)
-        w_scales = keep.tile([P, Q], U8, name="w_scales", align_bytes=64)
         nc.vector.tensor_tensor(out=w_bf[:], in0=p_turned[:].rearrange("s t q -> s q t"),
                                 in1=size_col[:].unsqueeze(1).to_broadcast([P, Q, PACK]), op=ALU.mult)
         nc.vector.reciprocal(inv_z[:], z_new[:])
-        nc.vector.quantize_mx(out=w_codes[:].bitcast(FP8X4), scales=w_scales[:],
-                              in_=w_bf[:].rearrange("p q j -> p (q j)"))
+        v_picked2 = pick(2, "v_picked2")
         nc.scalar.activation(old_share[:], r_old[:], ACT.Copy, scale=inv_z[:])
-        value_block(1)
-        value_block(2)
+        w_codes, w_scales = quantise("w", w_bf[:].rearrange("p q j -> p (q j)"), "v_raw2")
+
+        def product(dst, v_mx):
+            nc.tensor.matmul_mx(out=dst, lhsT=w_codes.bitcast(FP8X4), lhsT_scale=w_scales,
+                                rhs=v_mx[0].bitcast(FP8X4), rhs_scale=v_mx[1], start=True, stop=True)
+
+        def finish(name, o_new, cols, tag):
+            y = keep.tile([P, cols.stop - cols.start], F32, name=name, tag=tag, align_bytes=64)
+            nc.vector.scalar_tensor_tensor(out=y[:], in0=o_new[:], scalar=inv_z[:], in1=o_carried[:, cols],
+                                           op0=ALU.mult, op1=ALU.add)
+            nc.sync.dma_start(out=out[:, cols], in_=y[:])
 
         early = (BLOCKS - 1) * P
         o_early = psum.tile([P, early], F32, name="o_early")
         o_last = psum.tile([P, P], F32, name="o_last")
-        y_early = keep.tile([P, early], F32, name="y_early")
-        y_last = keep.tile([P, P], F32, name="y_last")
-
-        def product(dst, b):
-            nc.tensor.matmul_mx(out=dst, lhsT=w_codes[:].bitcast(FP8X4), lhsT_scale=w_scales[:],
-                                rhs=v_codes[b][:].bitcast(FP8X4), rhs_scale=v_scales[b][:], start=True, stop=True)
-
-        for b in range(BLOCKS - 1):
-            product(o_early[:, b * P : (b + 1) * P], b)
-        value_block(BLOCKS - 1)
+        v_bf2 = turn("2", [v_picked2], "turned2")
+        o_carried = keep.tile([P, E], F32, name="o_carried", tag="v_picked2", align_bytes=64)
         nc.scalar.activation(o_carried[:], o_old[:], ACT.Copy, scale=old_share[:])
-        nc.vector.scalar_tensor_tensor(out=y_early[:], in0=o_early[:], scalar=inv_z[:], in1=o_carried[:, :early],
-                                       op0=ALU.mult, op1=ALU.add)
-        nc.sync.dma_start(out=out[:, :early], in_=y_early[:])
-        product(o_last[:], BLOCKS - 1)
-        nc.vector.scalar_tensor_tensor(out=y_last[:], in0=o_last[:], scalar=inv_z[:], in1=o_carried[:, early:],
-                                       op0=ALU.mult, op1=ALU.add)
-        nc.sync.dma_start(out=out[:, early:], in_=y_last[:])
+        v_bf3 = turn("3", [pick(3, "v_picked3")], "turned3")
+        early_codes = keep.tile([P, early], U32, name="early_codes", tag="v_raw3", align_bytes=64)
+        early_scales = keep.tile([P, early], U8, name="early_scales", align_bytes=64)
+        for src, cols in ((v_bf01, slice(0, 2 * P)), (v_bf2, slice(2 * P, early))):
+            nc.vector.quantize_mx(out=early_codes[:, cols].bitcast(FP8X4), scales=early_scales[:, cols], in_=src[:])
+            product(o_early[:, cols], (early_codes[:, cols], early_scales[:, cols]))
+        product(o_last[:], quantise("v3", v_bf3[:], "v3_codes"))
+        finish("y_early", o_early, slice(0, early), "v_bf3")
+        finish("y_last", o_last, slice(early, E), "y_last")

@@ -19,6 +19,7 @@ ACT = mybir.ActivationFunctionType
 P = 128
 PACK = 4
 BLOCKS = E // P
+BANK = 512
 
 
 def tile_attend_resumedread_kernel(tc, query, keys_words, keys_scales, m0, z0, o0, size, vals, offs, out):
@@ -28,91 +29,85 @@ def tile_attend_resumedread_kernel(tc, query, keys_words, keys_scales, m0, z0, o
         psum = ctx.enter_context(tc.psum_pool(name="psum", bufs=1))
 
         key_words = keep.tile([P, T], U32, name="key_words", align_bytes=64)
-        key_scales = keep.tile([P, T], U8, name="key_scales", tag="key_scales", align_bytes=64)
+        key_scales = keep.tile([P, T], U8, name="key_scales", align_bytes=64)
         offsets = keep.tile([P, I // 16], U16, name="offsets")
         q_raw = keep.tile([P, PACK, Q], F32, name="q_raw")
         v_raw = [keep.tile([P, T], F32, name="v_raw%d" % b, tag="v_raw%d" % b, align_bytes=64) for b in range(BLOCKS)]
-        o_old = keep.tile([P, E], F32, name="o_old")
+        o_old = keep.tile([P, E], F32, name="o_old", tag="o_old", align_bytes=64)
         m_old = keep.tile([P, 1], F32, name="m_old")
         z_old = keep.tile([P, 1], F32, name="z_old")
-        size_col = keep.tile([P, PACK], F32, name="size_col")
+        size_col = keep.tile([P, PACK], F32, name="size_col", tag="size_col")
         ident = keep.tile([P, P], F32, name="ident")
-        warm = keep.tile([P, 1], F32, name="warm")
-        warm_out = keep.tile([P, 1], F32, name="warm_out")
 
         nc.vector.memset(key_scales[:].bitcast(I32), 0)
-        nc.vector.memset(warm[:], 0.0)
-        nc.scalar.activation(warm_out[:], warm[:], ACT.Exp)
 
+        nc.sync.dma_start(offsets[:], offs)
         nc.sync.dma_start(out=key_words[:].bitcast(I32),
                           in_=keys_words[0].rearrange("p n t -> p (n t)").bitcast(I32))
-        for quad in range(4):
-            nc.sync.dma_start(out=key_scales[32 * quad : 32 * quad + 4, :].bitcast(I32),
-                              in_=keys_scales[0, 4 * quad : 4 * quad + 4, :].bitcast(I32))
-        nc.sync.dma_start(offsets[:], offs)
+        for row in range(4):
+            nc.sync.dma_start(out=key_scales[row:P:32, :].bitcast(I32),
+                              in_=keys_scales[0, row:16:4, :].bitcast(I32))
         nc.sync.dma_start(out=q_raw[:], in_=query.rearrange("(p j) q -> p j q", j=PACK))
-        nc.sync.dma_start(out=v_raw[0][:], in_=vals[0:P, :])
+        for b in range(0, 1):
+            nc.sync.dma_start(out=v_raw[b][:], in_=vals[b * P : (b + 1) * P, :])
         nc.sync.dma_start(out=m_old[:], in_=m0)
         nc.sync.dma_start(out=size_col[:], in_=size[0].rearrange("(p j) -> p j", j=PACK))
         nc.sync.dma_start(out=z_old[:], in_=z0)
-        for b in range(1, BLOCKS):
+        for b in range(1, 4):
             nc.sync.dma_start(out=v_raw[b][:], in_=vals[b * P : (b + 1) * P, :])
         nc.sync.dma_start(out=o_old[:], in_=o0)
         make_identity(nc, ident[:])
 
         q_bf = keep.tile([P, Q, PACK], BF16, name="q_bf", align_bytes=64)
+        q_codes = keep.tile([P, Q], U32, name="q_codes", align_bytes=64)
         q_scales = keep.tile([P, Q], U8, name="q_scales", align_bytes=64)
         k_codes = keep.tile([P, I], U32, name="k_codes", align_bytes=64)
         k_scales = keep.tile([P, I], U8, name="k_scales", align_bytes=64)
         nc.scalar.copy(out=q_bf[:], in_=q_raw[:].rearrange("p j q -> p q j"))
-        nc.vector.tensor_copy(k_codes[:], key_words[:].indirect(offsets[:]))
         nc.vector.tensor_copy(k_scales[:], key_scales[:].indirect(offsets[:]))
-        q_codes = keep.tile([P, Q], U32, name="q_codes", align_bytes=64)
+        nc.vector.tensor_copy(k_codes[:], key_words[:].indirect(offsets[:]))
         nc.vector.quantize_mx(out=q_codes[:].bitcast(FP8X4), scales=q_scales[:],
                               in_=q_bf[:].rearrange("p q j -> p (q j)"))
 
-        scores = psum.tile([P, I], F32, name="scores", tag="turned0")
+        scores = psum.tile([P, I], F32, name="scores", tag="turned_even")
         nc.tensor.matmul_mx(out=scores[:], lhsT=q_codes[:].bitcast(FP8X4), lhsT_scale=q_scales[:],
                             rhs=k_codes[:].bitcast(FP8X4), rhs_scale=k_scales[:], start=True, stop=True)
 
-        neg_m_old = keep.tile([P, 1], F32, name="neg_m_old", tag="after_max2", align_bytes=64)
+        def pick(b):
+            v_picked = keep.tile([P, I], BF16, name="v_picked%d" % b, align_bytes=64)
+            nc.vector.tensor_copy(v_picked[:], v_raw[b][:].indirect(offsets[:]))
+            return v_picked
+
+        def turn(b, v_picked, v_bf, bank_tag):
+            pairs = v_picked[:].bitcast(F32)
+            turned = psum.tile([P, BANK], F32, name="turned%d" % b, tag=bank_tag)
+            for u in range(2):
+                nc.tensor.transpose(turned[:, u * P : (u + 1) * P], pairs[:, u : I // 2 : 2], ident[:])
+            nc.scalar.copy(out=v_bf.bitcast(F32).rearrange("p (e u) -> p e u", u=2),
+                           in_=turned[:, : 2 * P].rearrange("p (u e) -> p e u", u=2))
+
+        def quantise(name, v_bf, codes_tag):
+            width = v_bf.shape[1] // PACK
+            codes = keep.tile([P, width], U32, name="v_codes" + name, tag=codes_tag, align_bytes=64)
+            scales = keep.tile([P, width], U8, name="v_scales" + name, align_bytes=64)
+            nc.vector.quantize_mx(out=codes[:].bitcast(FP8X4), scales=scales[:], in_=v_bf)
+            return codes, scales
+
+        v_bf0 = keep.tile([P, I], BF16, name="v_bf0", tag="v_bf0", align_bytes=64)
+        v_bf12 = keep.tile([P, 2 * I], BF16, name="v_bf12", align_bytes=64)
+        turn(0, pick(0), v_bf0[:], "turned_odd")
+
+        score_max = keep.tile([P, 1], F32, name="score_max", tag="v_raw0", align_bytes=64)
         neg_m = keep.tile([P, 1], F32, name="neg_m")
-        neg_scores = keep.tile([P, I], BF16, name="neg_scores", tag="after_max", align_bytes=64)
         p_dealt = keep.tile([P, PACK, P], F32, name="p_dealt")
         p_sum = keep.tile([P, 1], F32, name="p_sum")
         decay = keep.tile([P, 1], F32, name="decay")
         r_old = keep.tile([P, 1], F32, name="r_old")
         z_new = keep.tile([P, 1], F32, name="z_new")
-        inv_z = keep.tile([P, 1], F32, name="inv_z")
         old_share = keep.tile([P, 1], F32, name="old_share")
-        nc.gpsimd.tensor_scalar(out=neg_m_old[:], in0=m_old[:], scalar1=-1.0, scalar2=0.0, op0=ALU.mult, op1=ALU.add)
-
-        def pick(b, picked_tag):
-            v_picked = keep.tile([P, I], BF16, name="v_picked%d" % b, tag=picked_tag, align_bytes=64)
-            nc.vector.tensor_copy(v_picked[:], v_raw[b][:].indirect(offsets[:]))
-            return v_picked
-
-        def turn(name, picked, bank_tag):
-            n = len(picked)
-            turned = psum.tile([P, n, 2, P], F32, name="turned" + name, tag=bank_tag)
-            for j, v_picked in enumerate(picked):
-                pairs = v_picked[:].bitcast(F32)
-                for u in range(2):
-                    nc.tensor.transpose(turned[:, j, u, :], pairs[:, u : I // 2 : 2], ident[:])
-            v_bf = keep.tile([P, n * P * PACK], BF16, name="v_bf" + name, tag="v_bf" + name, align_bytes=64)
-            nc.scalar.copy(out=v_bf[:].bitcast(F32).rearrange("p (j e u) -> p j e u", j=n, u=2),
-                           in_=turned[:].rearrange("p j u e -> p j e u"))
-            return v_bf
-
-        def quantise(name, src, codes_tag):
-            width = src.shape[1] // PACK
-            codes = keep.tile([P, width], U32, name=name + "_codes", tag=codes_tag, align_bytes=64)
-            scales = keep.tile([P, width], U8, name=name + "_scales", align_bytes=64)
-            nc.vector.quantize_mx(out=codes[:].bitcast(FP8X4), scales=scales[:], in_=src)
-            return codes[:], scales[:]
-
-        nc.vector.tensor_scalar(out=neg_scores[:], in0=scores[:], scalar1=-1.0, scalar2=neg_m_old[:],
-                                op0=ALU.mult, op1=ALU.min, accum_out=neg_m[:])
+        nc.vector.tensor_reduce(out=score_max[:], in_=scores[:], op=ALU.max, axis=mybir.AxisListType.X)
+        nc.vector.tensor_scalar(out=neg_m[:], in0=score_max[:], scalar1=m_old[:], scalar2=-1.0,
+                                op0=ALU.max, op1=ALU.mult)
         nc.scalar.activation(p_dealt[:], scores[:].rearrange("q (s t) -> q t s", t=PACK), ACT.Exp,
                              bias=neg_m[:], accum_out=p_sum[:])
         nc.scalar.activation(decay[:], m_old[:], ACT.Exp, bias=neg_m[:])
@@ -121,41 +116,44 @@ def tile_attend_resumedread_kernel(tc, query, keys_words, keys_scales, m0, z0, o
         p_turned = psum.tile([P, PACK, Q], F32, name="p_turned")
         for t in range(PACK):
             nc.tensor.transpose(p_turned[:, t, :], p_dealt[:, t, :], ident[:])
+        turn(1, pick(1), v_bf12[:, :I], "turned_even")
+        v_mx0 = quantise("0", v_bf0[:], "v_raw1")
 
-        v_picked0 = pick(0, "after_max")
-        v_picked1 = pick(1, "after_max2")
-        v_bf01 = turn("01", [v_picked0, v_picked1], "turned0")
-
-        w_bf = keep.tile([P, Q, PACK], BF16, name="w_bf", align_bytes=64)
+        w_bf = keep.tile([P, Q, PACK], BF16, name="w_bf", tag="v_bf0", align_bytes=64)
+        w_scales = keep.tile([P, Q], U8, name="w_scales", align_bytes=64)
         nc.vector.tensor_tensor(out=w_bf[:], in0=p_turned[:].rearrange("s t q -> s q t"),
                                 in1=size_col[:].unsqueeze(1).to_broadcast([P, Q, PACK]), op=ALU.mult)
+        inv_z = keep.tile([P, 1], F32, name="inv_z", tag="size_col")
         nc.vector.reciprocal(inv_z[:], z_new[:])
-        v_picked2 = pick(2, "v_picked2")
         nc.scalar.activation(old_share[:], r_old[:], ACT.Copy, scale=inv_z[:])
-        w_codes, w_scales = quantise("w", w_bf[:].rearrange("p q j -> p (q j)"), "v_raw2")
+        turn(2, pick(2), v_bf12[:, I:], "turned_odd")
+        w_codes = keep.tile([P, Q], U32, name="w_codes", tag="v_raw2", align_bytes=64)
+        nc.vector.quantize_mx(out=w_codes[:].bitcast(FP8X4), scales=w_scales[:],
+                              in_=w_bf[:].rearrange("p q j -> p (q j)"))
 
-        def product(dst, v_mx):
-            nc.tensor.matmul_mx(out=dst, lhsT=w_codes.bitcast(FP8X4), lhsT_scale=w_scales,
-                                rhs=v_mx[0].bitcast(FP8X4), rhs_scale=v_mx[1], start=True, stop=True)
+        def product(name, v_mx):
+            codes, scales = v_mx
+            width = codes.shape[1]
+            o_new = psum.tile([P, BANK], F32, name="o_new" + name)
+            nc.tensor.matmul_mx(out=o_new[:, :width], lhsT=w_codes[:].bitcast(FP8X4), lhsT_scale=w_scales[:],
+                                rhs=codes[:].bitcast(FP8X4), rhs_scale=scales[:], start=True, stop=True)
+            return o_new[:, :width]
+
+        o_new0 = product("0", v_mx0)
+        v_picked3 = pick(3)
+        o_carried = keep.tile([P, E], F32, name="o_carried")
+        nc.scalar.activation(o_carried[:], o_old[:], ACT.Copy, scale=old_share[:])
+        v_bf3 = keep.tile([P, I], BF16, name="v_bf3", tag="o_old", align_bytes=64)
+        turn(3, v_picked3, v_bf3[:], "turned_even")
+        o_new12 = product("12", quantise("12", v_bf12[:], "v_raw3"))
 
         def finish(name, o_new, cols, tag):
-            y = keep.tile([P, cols.stop - cols.start], F32, name=name, tag=tag, align_bytes=64)
-            nc.vector.scalar_tensor_tensor(out=y[:], in0=o_new[:], scalar=inv_z[:], in1=o_carried[:, cols],
+            y = keep.tile([P, cols.stop - cols.start], F32, name="y" + name, tag=tag, align_bytes=64)
+            nc.vector.scalar_tensor_tensor(out=y[:], in0=o_new, scalar=inv_z[:], in1=o_carried[:, cols],
                                            op0=ALU.mult, op1=ALU.add)
             nc.sync.dma_start(out=out[:, cols], in_=y[:])
 
-        early = (BLOCKS - 1) * P
-        o_early = psum.tile([P, early], F32, name="o_early")
-        o_last = psum.tile([P, P], F32, name="o_last")
-        v_bf2 = turn("2", [v_picked2], "turned2")
-        o_carried = keep.tile([P, E], F32, name="o_carried", tag="v_picked2", align_bytes=64)
-        nc.scalar.activation(o_carried[:], o_old[:], ACT.Copy, scale=old_share[:])
-        v_bf3 = turn("3", [pick(3, "v_picked3")], "turned3")
-        early_codes = keep.tile([P, early], U32, name="early_codes", tag="v_raw3", align_bytes=64)
-        early_scales = keep.tile([P, early], U8, name="early_scales", align_bytes=64)
-        for src, cols in ((v_bf01, slice(0, 2 * P)), (v_bf2, slice(2 * P, early))):
-            nc.vector.quantize_mx(out=early_codes[:, cols].bitcast(FP8X4), scales=early_scales[:, cols], in_=src[:])
-            product(o_early[:, cols], (early_codes[:, cols], early_scales[:, cols]))
-        product(o_last[:], quantise("v3", v_bf3[:], "v3_codes"))
-        finish("y_early", o_early, slice(0, early), "v_bf3")
-        finish("y_last", o_last, slice(early, E), "y_last")
+        finish("0", o_new0, slice(0, P), "y0")
+        o_new3 = product("3", quantise("3", v_bf3[:], "v_codes3"))
+        finish("12", o_new12, slice(P, 3 * P), "o_old")
+        finish("3", o_new3, slice(3 * P, E), "y3")

@@ -18,8 +18,14 @@ ACT = mybir.ActivationFunctionType
 
 P = 128
 PACK = 4
+PAIR = 2
+GROUP = 16
+QUADRANT = 32
+SCALE_RUN = 4
+SCALE_ROWS = D // 32
 BLOCKS = E // P
 BANK = 512
+ALIGN = 64
 
 
 def tile_attend_resumedread_kernel(tc, query, keys_words, keys_scales, m0, z0, o0, size, vals, offs, out):
@@ -28,15 +34,16 @@ def tile_attend_resumedread_kernel(tc, query, keys_words, keys_scales, m0, z0, o
         keep = ctx.enter_context(tc.tile_pool(name="keep", bufs=1))
         psum = ctx.enter_context(tc.psum_pool(name="psum", bufs=1))
 
-        key_words = keep.tile([P, T], U32, name="key_words", align_bytes=64)
-        key_scales = keep.tile([P, T], U8, name="key_scales", align_bytes=64)
-        offsets = keep.tile([P, I // 16], U16, name="offsets")
+        key_words = keep.tile([P, T], U32, name="key_words", align_bytes=ALIGN)
+        key_scales = keep.tile([P, T], U8, name="key_scales", align_bytes=ALIGN)
+        offsets = keep.tile([P, I // GROUP], U16, name="offsets")
         q_raw = keep.tile([P, PACK, Q], F32, name="q_raw")
-        v_raw = [keep.tile([P, T], F32, name="v_raw%d" % b, tag="v_raw%d" % b, align_bytes=64) for b in range(BLOCKS)]
-        o_old = keep.tile([P, E], F32, name="o_old", tag="o_old", align_bytes=64)
+        v_raw = [keep.tile([P, T], F32, name="v_raw%d" % b, tag="v_raw%d" % b, align_bytes=ALIGN)
+                 for b in range(BLOCKS)]
+        o_old = keep.tile([P, E], F32, name="o_old", tag="o_old", align_bytes=ALIGN)
         m_old = keep.tile([P, 1], F32, name="m_old")
         z_old = keep.tile([P, 1], F32, name="z_old")
-        size_col = keep.tile([P, PACK], F32, name="size_col", tag="size_col")
+        size_col = keep.tile([P, PACK], F32, name="size_col")
         ident = keep.tile([P, P], F32, name="ident")
 
         nc.vector.memset(key_scales[:].bitcast(I32), 0)
@@ -44,60 +51,59 @@ def tile_attend_resumedread_kernel(tc, query, keys_words, keys_scales, m0, z0, o
         nc.sync.dma_start(offsets[:], offs)
         nc.sync.dma_start(out=key_words[:].bitcast(I32),
                           in_=keys_words[0].rearrange("p n t -> p (n t)").bitcast(I32))
-        for row in range(4):
-            nc.sync.dma_start(out=key_scales[row:P:32, :].bitcast(I32),
-                              in_=keys_scales[0, row:16:4, :].bitcast(I32))
+        for row in range(SCALE_RUN):
+            nc.sync.dma_start(out=key_scales[row:P:QUADRANT, :].bitcast(I32),
+                              in_=keys_scales[0, row:SCALE_ROWS:SCALE_RUN, :].bitcast(I32))
         nc.sync.dma_start(out=q_raw[:], in_=query.rearrange("(p j) q -> p j q", j=PACK))
-        for b in range(0, 1):
-            nc.sync.dma_start(out=v_raw[b][:], in_=vals[b * P : (b + 1) * P, :])
+        nc.sync.dma_start(out=v_raw[0][:], in_=vals[0:P, :])
         nc.sync.dma_start(out=m_old[:], in_=m0)
         nc.sync.dma_start(out=size_col[:], in_=size[0].rearrange("(p j) -> p j", j=PACK))
         nc.sync.dma_start(out=z_old[:], in_=z0)
-        for b in range(1, 4):
+        for b in range(1, BLOCKS):
             nc.sync.dma_start(out=v_raw[b][:], in_=vals[b * P : (b + 1) * P, :])
         nc.sync.dma_start(out=o_old[:], in_=o0)
         make_identity(nc, ident[:])
 
-        q_bf = keep.tile([P, Q, PACK], BF16, name="q_bf", align_bytes=64)
-        q_codes = keep.tile([P, Q], U32, name="q_codes", align_bytes=64)
-        q_scales = keep.tile([P, Q], U8, name="q_scales", align_bytes=64)
-        k_codes = keep.tile([P, I], U32, name="k_codes", align_bytes=64)
-        k_scales = keep.tile([P, I], U8, name="k_scales", align_bytes=64)
+        q_bf = keep.tile([P, Q, PACK], BF16, name="q_bf", align_bytes=ALIGN)
+        q_codes = keep.tile([P, Q], U32, name="q_codes", align_bytes=ALIGN)
+        q_scales = keep.tile([P, Q], U8, name="q_scales", align_bytes=ALIGN)
+        k_codes = keep.tile([P, I], U32, name="k_codes", align_bytes=ALIGN)
+        k_scales = keep.tile([P, I], U8, name="k_scales", align_bytes=ALIGN)
         nc.scalar.copy(out=q_bf[:], in_=q_raw[:].rearrange("p j q -> p q j"))
         nc.vector.tensor_copy(k_scales[:], key_scales[:].indirect(offsets[:]))
         nc.vector.tensor_copy(k_codes[:], key_words[:].indirect(offsets[:]))
         nc.vector.quantize_mx(out=q_codes[:].bitcast(FP8X4), scales=q_scales[:],
                               in_=q_bf[:].rearrange("p q j -> p (q j)"))
 
-        scores = psum.tile([P, I], F32, name="scores", tag="turned_even")
+        scores = psum.tile([P, I], F32, name="scores", tag="bank_a")
         nc.tensor.matmul_mx(out=scores[:], lhsT=q_codes[:].bitcast(FP8X4), lhsT_scale=q_scales[:],
                             rhs=k_codes[:].bitcast(FP8X4), rhs_scale=k_scales[:], start=True, stop=True)
 
-        def pick(b):
-            v_picked = keep.tile([P, I], BF16, name="v_picked%d" % b, align_bytes=64)
+        def pick(b, picked_tag):
+            v_picked = keep.tile([P, I], BF16, name="v_picked%d" % b, tag=picked_tag, align_bytes=ALIGN)
             nc.vector.tensor_copy(v_picked[:], v_raw[b][:].indirect(offsets[:]))
             return v_picked
 
         def turn(b, v_picked, v_bf, bank_tag):
             pairs = v_picked[:].bitcast(F32)
             turned = psum.tile([P, BANK], F32, name="turned%d" % b, tag=bank_tag)
-            for u in range(2):
-                nc.tensor.transpose(turned[:, u * P : (u + 1) * P], pairs[:, u : I // 2 : 2], ident[:])
-            nc.scalar.copy(out=v_bf.bitcast(F32).rearrange("p (e u) -> p e u", u=2),
-                           in_=turned[:, : 2 * P].rearrange("p (u e) -> p e u", u=2))
+            for u in range(PAIR):
+                nc.tensor.transpose(turned[:, u * P : (u + 1) * P], pairs[:, u : I // PAIR : PAIR], ident[:])
+            nc.scalar.copy(out=v_bf.bitcast(F32).rearrange("p (e u) -> p e u", u=PAIR),
+                           in_=turned[:, : PAIR * P].rearrange("p (u e) -> p e u", u=PAIR))
 
         def quantise(name, v_bf, codes_tag):
             width = v_bf.shape[1] // PACK
-            codes = keep.tile([P, width], U32, name="v_codes" + name, tag=codes_tag, align_bytes=64)
-            scales = keep.tile([P, width], U8, name="v_scales" + name, align_bytes=64)
+            codes = keep.tile([P, width], U32, name="v_codes" + name, tag=codes_tag, align_bytes=ALIGN)
+            scales = keep.tile([P, width], U8, name="v_scales" + name, align_bytes=ALIGN)
             nc.vector.quantize_mx(out=codes[:].bitcast(FP8X4), scales=scales[:], in_=v_bf)
             return codes, scales
 
-        v_bf0 = keep.tile([P, I], BF16, name="v_bf0", tag="v_bf0", align_bytes=64)
-        v_bf12 = keep.tile([P, 2 * I], BF16, name="v_bf12", align_bytes=64)
-        turn(0, pick(0), v_bf0[:], "turned_odd")
+        v_bf0 = keep.tile([P, I], BF16, name="v_bf0", tag="v_bf0", align_bytes=ALIGN)
+        v_bf12 = keep.tile([P, 2 * I], BF16, name="v_bf12", align_bytes=ALIGN)
+        turn(0, pick(0, "v_picked0"), v_bf0[:], "bank_b")
 
-        score_max = keep.tile([P, 1], F32, name="score_max", tag="v_raw0", align_bytes=64)
+        score_max = keep.tile([P, 1], F32, name="score_max", tag="v_raw0", align_bytes=ALIGN)
         neg_m = keep.tile([P, 1], F32, name="neg_m")
         p_dealt = keep.tile([P, PACK, P], F32, name="p_dealt")
         p_sum = keep.tile([P, 1], F32, name="p_sum")
@@ -116,18 +122,19 @@ def tile_attend_resumedread_kernel(tc, query, keys_words, keys_scales, m0, z0, o
         p_turned = psum.tile([P, PACK, Q], F32, name="p_turned")
         for t in range(PACK):
             nc.tensor.transpose(p_turned[:, t, :], p_dealt[:, t, :], ident[:])
-        turn(1, pick(1), v_bf12[:, :I], "turned_even")
-        v_mx0 = quantise("0", v_bf0[:], "v_raw1")
 
-        w_bf = keep.tile([P, Q, PACK], BF16, name="w_bf", tag="v_bf0", align_bytes=64)
-        w_scales = keep.tile([P, Q], U8, name="w_scales", align_bytes=64)
-        nc.vector.tensor_tensor(out=w_bf[:], in0=p_turned[:].rearrange("s t q -> s q t"),
-                                in1=size_col[:].unsqueeze(1).to_broadcast([P, Q, PACK]), op=ALU.mult)
-        inv_z = keep.tile([P, 1], F32, name="inv_z", tag="size_col")
+        turn(1, pick(1, "v_raw0"), v_bf12[:, :I], "bank_a")
+        inv_z = keep.tile([P, 1], F32, name="inv_z", tag="v_raw1", align_bytes=ALIGN)
         nc.vector.reciprocal(inv_z[:], z_new[:])
         nc.scalar.activation(old_share[:], r_old[:], ACT.Copy, scale=inv_z[:])
-        turn(2, pick(2), v_bf12[:, I:], "turned_odd")
-        w_codes = keep.tile([P, Q], U32, name="w_codes", tag="v_raw2", align_bytes=64)
+        turn(2, pick(2, "v_picked2"), v_bf12[:, I:], "bank_b")
+
+        w_bf = keep.tile([P, Q, PACK], BF16, name="w_bf", tag="v_raw2", align_bytes=ALIGN)
+        nc.vector.tensor_tensor(out=w_bf[:], in0=p_turned[:].rearrange("s t q -> s q t"),
+                                in1=size_col[:].unsqueeze(1).to_broadcast([P, Q, PACK]), op=ALU.mult)
+        v_picked3 = pick(3, "v_picked3")
+        w_codes = keep.tile([P, Q], U32, name="w_codes", tag="v_raw3", align_bytes=ALIGN)
+        w_scales = keep.tile([P, Q], U8, name="w_scales", align_bytes=ALIGN)
         nc.vector.quantize_mx(out=w_codes[:].bitcast(FP8X4), scales=w_scales[:],
                               in_=w_bf[:].rearrange("p q j -> p (q j)"))
 
@@ -139,16 +146,15 @@ def tile_attend_resumedread_kernel(tc, query, keys_words, keys_scales, m0, z0, o
                                 rhs=codes[:].bitcast(FP8X4), rhs_scale=scales[:], start=True, stop=True)
             return o_new[:, :width]
 
-        o_new0 = product("0", v_mx0)
-        v_picked3 = pick(3)
         o_carried = keep.tile([P, E], F32, name="o_carried")
         nc.scalar.activation(o_carried[:], o_old[:], ACT.Copy, scale=old_share[:])
-        v_bf3 = keep.tile([P, I], BF16, name="v_bf3", tag="o_old", align_bytes=64)
-        turn(3, v_picked3, v_bf3[:], "turned_even")
-        o_new12 = product("12", quantise("12", v_bf12[:], "v_raw3"))
+        v_bf3 = keep.tile([P, I], BF16, name="v_bf3", tag="o_old", align_bytes=ALIGN)
+        turn(3, v_picked3, v_bf3[:], "bank_a")
+        o_new0 = product("0", quantise("0", v_bf0[:], "v_raw2"))
+        o_new12 = product("12", quantise("12", v_bf12[:], "v_bf0"))
 
-        def finish(name, o_new, cols, tag):
-            y = keep.tile([P, cols.stop - cols.start], F32, name="y" + name, tag=tag, align_bytes=64)
+        def finish(name, o_new, cols, y_tag):
+            y = keep.tile([P, cols.stop - cols.start], F32, name="y" + name, tag=y_tag, align_bytes=ALIGN)
             nc.vector.scalar_tensor_tensor(out=y[:], in0=o_new, scalar=inv_z[:], in1=o_carried[:, cols],
                                            op0=ALU.mult, op1=ALU.add)
             nc.sync.dma_start(out=out[:, cols], in_=y[:])

from contextlib import ExitStack

import concourse.mybir as mybir
from concourse.masks import make_identity

D, T, I, Q, E = 512, 2048, 512, 128, 512
FLOPS = 2 * D * Q * I + 2 * I * Q * E

F32 = mybir.dt.float32
BF16 = mybir.dt.bfloat16
I32 = mybir.dt.int32
U32 = mybir.dt.uint32
U16 = mybir.dt.uint16
U8 = mybir.dt.uint8
FP8X4 = mybir.dt.float8_e4m3fn_x4
ALU = mybir.AluOpType
ACT = mybir.ActivationFunctionType

P = 128
PACK = 4
PAIR = 2
GROUP = 16
QUADRANT = 32
SCALE_RUN = 4
SCALE_ROWS = D // 32
BLOCKS = E // P
BANK = 512
ALIGN = 64


def tile_attend_resumedread_kernel(tc, query, keys_words, keys_scales, m0, z0, o0, size, vals, offs, out):
    nc = tc.nc
    with ExitStack() as ctx:
        keep = ctx.enter_context(tc.tile_pool(name="keep", bufs=1))
        psum = ctx.enter_context(tc.psum_pool(name="psum", bufs=1))

        key_words = keep.tile([P, T], U32, name="key_words", align_bytes=ALIGN)
        key_scales = keep.tile([P, T], U8, name="key_scales", align_bytes=ALIGN)
        offsets = keep.tile([P, I // GROUP], U16, name="offsets")
        q_raw = keep.tile([P, PACK, Q], F32, name="q_raw")
        v_raw = [keep.tile([P, T], F32, name="v_raw%d" % b, tag="v_raw%d" % b, align_bytes=ALIGN)
                 for b in range(BLOCKS)]
        o_old = keep.tile([P, E], F32, name="o_old", tag="o_old", align_bytes=ALIGN)
        m_old = keep.tile([P, 1], F32, name="m_old")
        z_old = keep.tile([P, 1], F32, name="z_old")
        size_col = keep.tile([P, PACK], F32, name="size_col")
        ident = keep.tile([P, P], F32, name="ident")

        nc.vector.memset(key_scales[:].bitcast(I32), 0)

        nc.sync.dma_start(offsets[:], offs)
        nc.sync.dma_start(out=key_words[:].bitcast(I32),
                          in_=keys_words[0].rearrange("p n t -> p (n t)").bitcast(I32))
        for row in range(SCALE_RUN):
            nc.sync.dma_start(out=key_scales[row:P:QUADRANT, :].bitcast(I32),
                              in_=keys_scales[0, row:SCALE_ROWS:SCALE_RUN, :].bitcast(I32))
        nc.sync.dma_start(out=q_raw[:], in_=query.rearrange("(p j) q -> p j q", j=PACK))
        nc.sync.dma_start(out=v_raw[0][:], in_=vals[0:P, :])
        nc.sync.dma_start(out=m_old[:], in_=m0)
        nc.sync.dma_start(out=size_col[:], in_=size[0].rearrange("(p j) -> p j", j=PACK))
        nc.sync.dma_start(out=z_old[:], in_=z0)
        for b in range(1, BLOCKS):
            nc.sync.dma_start(out=v_raw[b][:], in_=vals[b * P : (b + 1) * P, :])
        nc.sync.dma_start(out=o_old[:], in_=o0)
        make_identity(nc, ident[:])

        q_bf = keep.tile([P, Q, PACK], BF16, name="q_bf", align_bytes=ALIGN)
        q_codes = keep.tile([P, Q], U32, name="q_codes", align_bytes=ALIGN)
        q_scales = keep.tile([P, Q], U8, name="q_scales", align_bytes=ALIGN)
        k_codes = keep.tile([P, I], U32, name="k_codes", align_bytes=ALIGN)
        k_scales = keep.tile([P, I], U8, name="k_scales", align_bytes=ALIGN)
        nc.scalar.copy(out=q_bf[:], in_=q_raw[:].rearrange("p j q -> p q j"))
        nc.vector.tensor_copy(k_scales[:], key_scales[:].indirect(offsets[:]))
        nc.vector.tensor_copy(k_codes[:], key_words[:].indirect(offsets[:]))
        nc.vector.quantize_mx(out=q_codes[:].bitcast(FP8X4), scales=q_scales[:],
                              in_=q_bf[:].rearrange("p q j -> p (q j)"))

        scores = psum.tile([P, I], F32, name="scores", tag="bank_a")
        nc.tensor.matmul_mx(out=scores[:], lhsT=q_codes[:].bitcast(FP8X4), lhsT_scale=q_scales[:],
                            rhs=k_codes[:].bitcast(FP8X4), rhs_scale=k_scales[:], start=True, stop=True)

        def pick(b, picked_tag):
            v_picked = keep.tile([P, I], BF16, name="v_picked%d" % b, tag=picked_tag, align_bytes=ALIGN)
            nc.vector.tensor_copy(v_picked[:], v_raw[b][:].indirect(offsets[:]))
            return v_picked

        def turn(b, v_picked, v_bf, bank_tag):
            pairs = v_picked[:].bitcast(F32)
            turned = psum.tile([P, BANK], F32, name="turned%d" % b, tag=bank_tag)
            for u in range(PAIR):
                nc.tensor.transpose(turned[:, u * P : (u + 1) * P], pairs[:, u : I // PAIR : PAIR], ident[:])
            nc.scalar.copy(out=v_bf.bitcast(F32).rearrange("p (e u) -> p e u", u=PAIR),
                           in_=turned[:, : PAIR * P].rearrange("p (u e) -> p e u", u=PAIR))

        def quantise(name, v_bf, codes_tag):
            width = v_bf.shape[1] // PACK
            codes = keep.tile([P, width], U32, name="v_codes" + name, tag=codes_tag, align_bytes=ALIGN)
            scales = keep.tile([P, width], U8, name="v_scales" + name, align_bytes=ALIGN)
            nc.vector.quantize_mx(out=codes[:].bitcast(FP8X4), scales=scales[:], in_=v_bf)
            return codes, scales

        v_bf0 = keep.tile([P, I], BF16, name="v_bf0", tag="v_bf0", align_bytes=ALIGN)
        v_bf12 = keep.tile([P, 2 * I], BF16, name="v_bf12", align_bytes=ALIGN)
        turn(0, pick(0, "v_picked0"), v_bf0[:], "bank_b")

        score_max = keep.tile([P, 1], F32, name="score_max", tag="v_raw0", align_bytes=ALIGN)
        neg_m = keep.tile([P, 1], F32, name="neg_m")
        p_dealt = keep.tile([P, PACK, P], F32, name="p_dealt")
        p_sum = keep.tile([P, 1], F32, name="p_sum")
        decay = keep.tile([P, 1], F32, name="decay")
        r_old = keep.tile([P, 1], F32, name="r_old")
        z_new = keep.tile([P, 1], F32, name="z_new")
        old_share = keep.tile([P, 1], F32, name="old_share")
        nc.vector.tensor_reduce(out=score_max[:], in_=scores[:], op=ALU.max, axis=mybir.AxisListType.X)
        nc.vector.tensor_scalar(out=neg_m[:], in0=score_max[:], scalar1=m_old[:], scalar2=-1.0,
                                op0=ALU.max, op1=ALU.mult)
        nc.scalar.activation(p_dealt[:], scores[:].rearrange("q (s t) -> q t s", t=PACK), ACT.Exp,
                             bias=neg_m[:], accum_out=p_sum[:])
        nc.scalar.activation(decay[:], m_old[:], ACT.Exp, bias=neg_m[:])
        nc.scalar.activation(r_old[:], decay[:], ACT.Copy, scale=z_old[:])
        nc.scalar.activation(z_new[:], decay[:], ACT.Identity, bias=p_sum[:], scale=z_old[:])
        p_turned = psum.tile([P, PACK, Q], F32, name="p_turned")
        for t in range(PACK):
            nc.tensor.transpose(p_turned[:, t, :], p_dealt[:, t, :], ident[:])

        turn(1, pick(1, "v_raw0"), v_bf12[:, :I], "bank_a")
        inv_z = keep.tile([P, 1], F32, name="inv_z", tag="v_raw1", align_bytes=ALIGN)
        nc.vector.reciprocal(inv_z[:], z_new[:])
        nc.scalar.activation(old_share[:], r_old[:], ACT.Copy, scale=inv_z[:])
        turn(2, pick(2, "v_picked2"), v_bf12[:, I:], "bank_b")

        w_bf = keep.tile([P, Q, PACK], BF16, name="w_bf", tag="v_raw2", align_bytes=ALIGN)
        nc.vector.tensor_tensor(out=w_bf[:], in0=p_turned[:].rearrange("s t q -> s q t"),
                                in1=size_col[:].unsqueeze(1).to_broadcast([P, Q, PACK]), op=ALU.mult)
        v_picked3 = pick(3, "v_picked3")
        w_codes = keep.tile([P, Q], U32, name="w_codes", tag="v_raw3", align_bytes=ALIGN)
        w_scales = keep.tile([P, Q], U8, name="w_scales", align_bytes=ALIGN)
        nc.vector.quantize_mx(out=w_codes[:].bitcast(FP8X4), scales=w_scales[:],
                              in_=w_bf[:].rearrange("p q j -> p (q j)"))

        def product(name, v_mx):
            codes, scales = v_mx
            width = codes.shape[1]
            o_new = psum.tile([P, BANK], F32, name="o_new" + name)
            nc.tensor.matmul_mx(out=o_new[:, :width], lhsT=w_codes[:].bitcast(FP8X4), lhsT_scale=w_scales[:],
                                rhs=codes[:].bitcast(FP8X4), rhs_scale=scales[:], start=True, stop=True)
            return o_new[:, :width]

        o_carried = keep.tile([P, E], F32, name="o_carried")
        nc.scalar.activation(o_carried[:], o_old[:], ACT.Copy, scale=old_share[:])
        v_bf3 = keep.tile([P, I], BF16, name="v_bf3", tag="o_old", align_bytes=ALIGN)
        turn(3, v_picked3, v_bf3[:], "bank_a")
        o_new0 = product("0", quantise("0", v_bf0[:], "v_raw2"))
        o_new12 = product("12", quantise("12", v_bf12[:], "v_bf0"))

        def finish(name, o_new, cols, y_tag):
            y = keep.tile([P, cols.stop - cols.start], F32, name="y" + name, tag=y_tag, align_bytes=ALIGN)
            nc.vector.scalar_tensor_tensor(out=y[:], in0=o_new, scalar=inv_z[:], in1=o_carried[:, cols],
                                           op0=ALU.mult, op1=ALU.add)
            nc.sync.dma_start(out=out[:, cols], in_=y[:])

        finish("0", o_new0, slice(0, P), "y0")
        o_new3 = product("3", quantise("3", v_bf3[:], "v_codes3"))
        finish("12", o_new12, slice(P, 3 * P), "o_old")
        finish("3", o_new3, slice(3 * P, E), "y3")
